import numpy as np
import ml_dtypes


def mxq(x, axis, fmt="e4m3"):
    dtype, down = {"e4m3": (ml_dtypes.float8_e4m3fn, 7), "e5m2": (ml_dtypes.float8_e5m2, 14)}[fmt]
    v = np.moveaxis(np.asarray(x, np.float32).astype(ml_dtypes.bfloat16).astype(np.float64), axis, -1)
    blocks = v.reshape(v.shape[:-1] + (-1, 32))
    amax = np.abs(blocks).max(-1, keepdims=True)
    byte = np.maximum(np.where(amax > 0, np.frexp(amax)[1] - 1 + 127, 0) - down, 1)
    scale = np.exp2(byte - 127.0)
    codes = (blocks / scale).astype(np.float32).astype(dtype).astype(np.float64)
    return np.moveaxis((codes * scale).reshape(v.shape), -1, axis)


WIDE = False


def mx_kscale(k):
    if not WIDE:
        return np.ones(k)
    levels = np.array([10, -10, 5, -5, 0])
    if k % 512:
        return np.exp2(np.random.permutation(np.resize(levels, k // 32))).repeat(32)
    a = np.empty((k // 512, 16))
    for p in range(k // 512):
        a[p, :8] = np.random.permutation(np.resize(levels, 8))
        for g in range(8):
            far = levels[np.abs(levels - a[p, g]) >= 10]
            a[p, g + 8] = far[np.random.randint(len(far))]
    return np.exp2(a.ravel()).repeat(32)


def f64(x):
    return np.asarray(x).astype(np.float64)


def striped(idx):
    return np.tile(idx.reshape(-1, 16).T, (8, 1)).astype(np.uint16)


def unstriped(offs):
    return offs[:16].T.reshape(-1).astype(np.int64)


def striped8(idx):
    return np.concatenate([v.reshape(-1, 16).T for v in idx]).astype(np.uint16)


def unstriped8(offs):
    return np.stack([offs[16 * g:16 * g + 16].T.reshape(-1) for g in range(8)]).astype(np.int64)


E2M1 = np.array([0.0, 0.5, 1.0, 1.5, 2.0, 3.0, 4.0, 6.0, -0.0, -0.5, -1.0, -1.5, -2.0, -3.0, -4.0, -6.0])


def pack_weight(w, fmt):
    k, n = w.shape
    w = f64(np.asarray(w, np.float32).astype(ml_dtypes.bfloat16)).reshape(k // 32, 32, n)
    amax = np.abs(w).max(1)
    if fmt == "e4m3":
        byte = np.frexp(amax)[1] - 1 + 127 - 7
    else:
        mant, ex = np.frexp(amax / 6.0)
        byte = np.where(mant > 0.5, ex, ex - 1) + 127
    byte = np.clip(np.where(amax > 0, byte, 1), 1, 254)
    scaled = (w * np.exp2(127.0 - byte)[:, None, :]).reshape(k, n).astype(np.float32)
    by_word = np.ascontiguousarray(scaled.reshape(k // 512, 128, 4, n).transpose(0, 1, 3, 2))
    if fmt == "e4m3":
        words = by_word.astype(ml_dtypes.float8_e4m3fn).view(np.uint8)
    else:
        c = by_word.astype(ml_dtypes.float4_e2m1fn).view(np.uint8) & 0xF
        words = (c[..., 0::2] | (c[..., 1::2] << 4)).reshape(k // 512, 128, 2 * n)
    return np.ascontiguousarray(words), np.ascontiguousarray(byte.astype(np.uint8).reshape(k // 512, 16, n))


def unpack_weight(words, scales, fmt):
    g, _, n = scales.shape
    words = np.ascontiguousarray(words).reshape(g, 128, n, -1)
    if fmt == "e4m3":
        vals = words.view(ml_dtypes.float8_e4m3fn).astype(np.float64)
    else:
        nib = np.empty((g, 128, n, 4), np.uint8)
        nib[..., 0::2] = words & 0xF
        nib[..., 1::2] = words >> 4
        vals = E2M1[nib]
    vals = vals * np.repeat(np.exp2(scales.astype(np.float64) - 127.0), 8, axis=1)[..., None]
    return vals.transpose(0, 1, 3, 2).reshape(g * 512, n)


def pack_table(v):
    words, scales = pack_weight(v, "e4m3")
    return np.concatenate([words.reshape(words.shape[0], -1), scales.reshape(scales.shape[0], -1)], axis=1)


def unpack_table(tab):
    g, t = tab.shape[0], tab.shape[1] // 528
    return unpack_weight(tab[:, :512 * t].reshape(g, 128, t, 4), tab[:, 512 * t:].reshape(g, 16, t), "e4m3")


K, M, T, S = 1024, 256, 2048, 1024


def setup_inputs():
    n = np.random.standard_normal
    s = mx_kscale(K)[:, None]
    w = n((K, M)) / np.sqrt(K) / s
    p_w4 = pack_weight(w[512:], "e2m1")
    return {
        "tab": pack_table(n((K, T)) * s),
        "w8": (w[:512]).astype(np.float32),
        "w4_words": p_w4[0],
        "w4_scales": p_w4[1],
        "b": (0.3 * n(256)).astype(np.float32),
        "wgo": np.repeat(np.random.uniform(0.5, 2.0, (8, S)), 16, axis=0).astype(np.float32),
        "offs": striped(np.random.permutation(T)[:S]),
        "offs2": striped8(np.stack([np.random.permutation(T)[:S] for _ in range(8)])),
    }


def reference(tab, w8, w4_words, w4_scales, b, wgo, offs, offs2):
    tab_ = unpack_table(tab)[:, unstriped(offs)]
    w8_ = mxq(f64(w8), 0, "e4m3")
    w4_ = unpack_weight(w4_words, w4_scales, "e2m1")
    y = w8_.T @ tab_[:512] + w4_.T @ tab_[512:]
    place = unstriped8(offs2)[np.arange(M) % 128 // 16]
    out = np.zeros((M, T))
    out[np.arange(M)[:, None], place] = f64(wgo)[np.arange(M) % 128] * (y + f64(b)[:, None])
    return out

@@ -1,0 +1,131 @@
+from contextlib import ExitStack
+
+import concourse.mybir as mybir
+
+K, M, T, S = 1024, 256, 2048, 1024
+FLOPS = 2 * K * M * S
+
+F32 = mybir.dt.float32
+BF16 = mybir.dt.bfloat16
+I32 = mybir.dt.int32
+U32 = mybir.dt.uint32
+U16 = mybir.dt.uint16
+U8 = mybir.dt.uint8
+FP8X4 = mybir.dt.float8_e4m3fn_x4
+FP4X4 = mybir.dt.float4_e2m1fn_x4
+
+P = 128
+PACK = 4
+QUADS = 4
+QROWS = 4
+N = 512
+HALVES = S // N
+ROWT = M // P
+WORD_BYTES = P * PACK * T
+LCOL = N // 16
+
+
+def tile_list_tabhs_o_bias_kernel(tc, tab, w8, w4_words, w4_scales, b, wgo, offs, offs2, out):
+    nc = tc.nc
+    with ExitStack() as ctx:
+        lists = ctx.enter_context(tc.tile_pool(name="lists", bufs=1))
+        keep = ctx.enter_context(tc.tile_pool(name="keep", bufs=1))
+        psum = ctx.enter_context(tc.psum_pool(name="psum", bufs=1))
+
+        pick = lists.tile([P, S // 16], U16, name="pick")
+        place = lists.tile([P, S // 16], U16, name="place")
+
+        tab_scale = keep.tile([P, T], U8, name="tab_scale", align_bytes=64)
+        tab_words = [keep.tile([P, T], I32, name="tab_words%d" % a, align_bytes=64) for a in range(2)]
+        w8_raw = keep.tile([P, PACK, M], F32, name="w8_raw", align_bytes=64)
+        wgo_sb = keep.tile([P, S], F32, name="wgo_sb", align_bytes=64)
+        w4_code = keep.tile([P, 2 * M], U8, name="w4_code", align_bytes=64)
+        w4_plane = keep.tile([P, M], U8, name="w4_plane", align_bytes=64)
+        bias = keep.tile([P, ROWT], F32, name="bias", align_bytes=64)
+        planes = keep.tile([P, 2, S], U8, name="planes", align_bytes=64)
+        pages = [keep.tile([P, T], F32, name="page%d" % m, align_bytes=64) for m in range(ROWT)]
+
+        nc.vector.memset(tab_scale[32:64, :].bitcast(I32), 0)
+        nc.vector.memset(tab_scale[64:128, :].bitcast(I32), 0)
+        nc.gpsimd.memset(w4_plane[:].bitcast(I32), 0)
+        nc.gpsimd.memset(planes[:].bitcast(I32), 0)
+        nc.vector.memset(pages[0][:].bitcast(I32), 0)
+
+        def words_of(a):
+            return tab[a, 0:WORD_BYTES].rearrange("(p t) -> p t", p=P).bitcast(I32)
+
+        nc.sync.dma_start(pick[:], offs)
+        scale_rows = tab[:, WORD_BYTES:].bitcast(I32).rearrange("a (q c) -> q a c", q=QUADS * QROWS)
+        nc.sync.dma_start(tab_scale[0:32, :].bitcast(I32), scale_rows)
+        nc.sync.dma_start(tab_words[0][:], words_of(0))
+        nc.sync.dma_start(w8_raw[:], w8.rearrange("(p j) n -> p j n", j=PACK))
+        nc.sync.dma_start(tab_words[1][:], words_of(1))
+        nc.sync.dma_start(w4_code[:].bitcast(I32), w4_words[0].bitcast(I32))
+        nc.sync.dma_start(place[:], offs2)
+        nc.sync.dma_start(wgo_sb[:], wgo)
+        for q in range(QUADS):
+            nc.gpsimd.dma_start(
+                w4_plane[32 * q : 32 * q + QROWS, :].bitcast(I32),
+                w4_scales[0, QROWS * q : QROWS * (q + 1), :].bitcast(I32),
+            )
+        with nc.allow_non_contiguous_dma(reason="one bias value for each partition and row tile"):
+            nc.gpsimd.dma_start(bias[:], b.rearrange("(m p) -> p m", p=P))
+        nc.gpsimd.memset(pages[1][:].bitcast(I32), 0)
+
+        got_scale = keep.tile([P, S], U8, name="got_scale", align_bytes=64)
+        nc.vector.tensor_copy(got_scale[:], tab_scale[:].indirect(pick[:]))
+        for q in range(QUADS):
+            nc.scalar.dma_start(
+                planes[32 * q : 32 * q + QROWS, :, :].bitcast(I32),
+                got_scale[2 * QROWS * q : 2 * QROWS * (q + 1), :].bitcast(I32),
+            )
+
+        got0 = keep.tile([P, S], U32, name="got0", align_bytes=64)
+        nc.vector.tensor_copy(got0[:], tab_words[0][:].bitcast(U32).indirect(pick[:]))
+
+        w8_bf = keep.tile([P, M, PACK], BF16, name="w8_bf", tag="shared", align_bytes=64)
+        nc.scalar.copy(w8_bf[:], w8_raw[:].rearrange("p j n -> p n j"))
+        w8_code = keep.tile([P, M], U32, name="w8_code", align_bytes=64)
+        w8_plane = keep.tile([P, M], U8, name="w8_plane", align_bytes=64)
+        nc.vector.quantize_mx(out=w8_code[:].bitcast(FP8X4), scales=w8_plane[:], in_=w8_bf[:].rearrange("p n j -> p (n j)"))
+
+        got1 = []
+        for h in range(HALVES):
+            g = keep.tile([P, N], U32, name="got1_%d" % h, tag="shared" if h == 0 else "got1_last", align_bytes=64)
+            nc.vector.tensor_copy(g[:], tab_words[1][:].bitcast(U32).indirect(pick[:, h * LCOL : (h + 1) * LCOL]))
+            got1.append(g)
+
+        acc = {}
+        for h in range(HALVES):
+            cols = slice(h * N, (h + 1) * N)
+            for m in range(ROWT):
+                rows = slice(m * P, (m + 1) * P)
+                acc[h, m] = psum.tile([P, N], F32, name="acc%d%d" % (h, m))
+                nc.tensor.matmul_mx(
+                    out=acc[h, m][:],
+                    lhsT=w8_code[:, rows].bitcast(FP8X4),
+                    lhsT_scale=w8_plane[:, rows],
+                    rhs=got0[:, cols].bitcast(FP8X4),
+                    rhs_scale=planes[:, 0, cols],
+                    start=True,
+                    stop=False,
+                )
+                nc.tensor.matmul_mx(
+                    out=acc[h, m][:],
+                    lhsT=w4_code[:, 2 * m * P : 2 * (m + 1) * P].bitcast(FP4X4),
+                    lhsT_scale=w4_plane[:, rows],
+                    rhs=got1[h][:].bitcast(FP8X4),
+                    rhs_scale=planes[:, 1, cols],
+                    start=False,
+                    stop=True,
+                )
+                y = keep.tile([P, N], F32, name="y%d%d" % (h, m), align_bytes=64)
+                nc.scalar.activation(y[:], acc[h, m][:], mybir.ActivationFunctionType.Identity, bias=bias[:, m : m + 1])
+                nc.vector.tensor_tensor(
+                    pages[m][:].indirect(place[:, h * LCOL : (h + 1) * LCOL]),
+                    y[:],
+                    wgo_sb[:, cols],
+                    mybir.AluOpType.mult,
+                )
+        for m in range(ROWT):
+            nc.sync.dma_start(out[m * P : (m + 1) * P, :], pages[m][:])

@@ -22,7 +22,17 @@ N = 512
 HALVES = S // N
 ROWT = M // P
 WORD_BYTES = P * PACK * T
-LCOL = N // 16
+SHORT = 128
+CHUNKS = ((0, 256), (256, S))
+
+
+def banks_of(lo, hi):
+    return [(c, min(c + N, hi)) for c in range(lo, hi, N)]
+
+
+def passes_of(lo, hi):
+    step = N if hi - lo == N else SHORT
+    return [(c, c + step) for c in range(lo, hi, step)]
 
 
 def tile_list_tabhs_o_bias_kernel(tc, tab, w8, w4_words, w4_scales, b, wgo, offs, offs2, out):
@@ -35,10 +45,9 @@ def tile_list_tabhs_o_bias_kernel(tc, tab, w8, w4_words, w4_scales, b, wgo, offs
         pick = lists.tile([P, S // 16], U16, name="pick")
         place = lists.tile([P, S // 16], U16, name="place")
 
-        tab_scale = keep.tile([P, T], U8, name="tab_scale", align_bytes=64)
+        tab_scale = keep.tile([P, T], U8, name="tab_scale", tag="late", align_bytes=64)
         tab_words = [keep.tile([P, T], I32, name="tab_words%d" % a, align_bytes=64) for a in range(2)]
         w8_raw = keep.tile([P, PACK, M], F32, name="w8_raw", align_bytes=64)
-        wgo_sb = keep.tile([P, S], F32, name="wgo_sb", align_bytes=64)
         w4_code = keep.tile([P, 2 * M], U8, name="w4_code", align_bytes=64)
         w4_plane = keep.tile([P, M], U8, name="w4_plane", align_bytes=64)
         bias = keep.tile([P, ROWT], F32, name="bias", align_bytes=64)
@@ -51,6 +60,10 @@ def tile_list_tabhs_o_bias_kernel(tc, tab, w8, w4_words, w4_scales, b, wgo, offs
         nc.gpsimd.memset(planes[:].bitcast(I32), 0)
         nc.vector.memset(pages[0][:].bitcast(I32), 0)
 
+        warm = keep.tile([P, 2], F32, name="warm")
+        nc.gpsimd.memset(warm[:, 0:1], 0.0)
+        nc.scalar.activation(warm[:, 1:2], warm[:, 0:1], mybir.ActivationFunctionType.Identity, bias=warm[:, 0:1])
+
         def words_of(a):
             return tab[a, 0:WORD_BYTES].rearrange("(p t) -> p t", p=P).bitcast(I32)
 
@@ -62,7 +75,6 @@ def tile_list_tabhs_o_bias_kernel(tc, tab, w8, w4_words, w4_scales, b, wgo, offs
         nc.sync.dma_start(tab_words[1][:], words_of(1))
         nc.sync.dma_start(w4_code[:].bitcast(I32), w4_words[0].bitcast(I32))
         nc.sync.dma_start(place[:], offs2)
-        nc.sync.dma_start(wgo_sb[:], wgo)
         for q in range(QUADS):
             nc.gpsimd.dma_start(
                 w4_plane[32 * q : 32 * q + QROWS, :].bitcast(I32),
@@ -75,10 +87,13 @@ def tile_list_tabhs_o_bias_kernel(tc, tab, w8, w4_words, w4_scales, b, wgo, offs
         got_scale = keep.tile([P, S], U8, name="got_scale", align_bytes=64)
         nc.vector.tensor_copy(got_scale[:], tab_scale[:].indirect(pick[:]))
         for q in range(QUADS):
-            nc.scalar.dma_start(
+            nc.sync.dma_start(
                 planes[32 * q : 32 * q + QROWS, :, :].bitcast(I32),
                 got_scale[2 * QROWS * q : 2 * QROWS * (q + 1), :].bitcast(I32),
             )
+
+        wgo_sb = keep.tile([P, S], F32, name="wgo_sb", tag="late", align_bytes=64)
+        nc.sync.dma_start(wgo_sb[:], wgo)
 
         got0 = keep.tile([P, S], U32, name="got0", align_bytes=64)
         nc.vector.tensor_copy(got0[:], tab_words[0][:].bitcast(U32).indirect(pick[:]))
@@ -90,41 +105,43 @@ def tile_list_tabhs_o_bias_kernel(tc, tab, w8, w4_words, w4_scales, b, wgo, offs
         nc.vector.quantize_mx(out=w8_code[:].bitcast(FP8X4), scales=w8_plane[:], in_=w8_bf[:].rearrange("p n j -> p (n j)"))
 
         got1 = []
-        for h in range(HALVES):
-            g = keep.tile([P, N], U32, name="got1_%d" % h, tag="shared" if h == 0 else "got1_last", align_bytes=64)
-            nc.vector.tensor_copy(g[:], tab_words[1][:].bitcast(U32).indirect(pick[:, h * LCOL : (h + 1) * LCOL]))
+        for h, (lo, hi) in enumerate(CHUNKS):
+            g = keep.tile([P, hi - lo], U32, name="got1_%d" % h, tag="shared" if h == 0 else "got1_last", align_bytes=64)
+            nc.vector.tensor_copy(g[:], tab_words[1][:].bitcast(U32).indirect(pick[:, lo // 16 : hi // 16]))
             got1.append(g)
 
-        acc = {}
-        for h in range(HALVES):
-            cols = slice(h * N, (h + 1) * N)
+        for h, (lo, hi) in enumerate(CHUNKS):
             for m in range(ROWT):
                 rows = slice(m * P, (m + 1) * P)
-                acc[h, m] = psum.tile([P, N], F32, name="acc%d%d" % (h, m))
-                nc.tensor.matmul_mx(
-                    out=acc[h, m][:],
-                    lhsT=w8_code[:, rows].bitcast(FP8X4),
-                    lhsT_scale=w8_plane[:, rows],
-                    rhs=got0[:, cols].bitcast(FP8X4),
-                    rhs_scale=planes[:, 0, cols],
-                    start=True,
-                    stop=False,
-                )
-                nc.tensor.matmul_mx(
-                    out=acc[h, m][:],
-                    lhsT=w4_code[:, 2 * m * P : 2 * (m + 1) * P].bitcast(FP4X4),
-                    lhsT_scale=w4_plane[:, rows],
-                    rhs=got1[h][:].bitcast(FP8X4),
-                    rhs_scale=planes[:, 1, cols],
-                    start=False,
-                    stop=True,
-                )
-                y = keep.tile([P, N], F32, name="y%d%d" % (h, m), align_bytes=64)
-                nc.scalar.activation(y[:], acc[h, m][:], mybir.ActivationFunctionType.Identity, bias=bias[:, m : m + 1])
+                y = keep.tile([P, hi - lo], F32, name="y%d%d" % (h, m), align_bytes=64)
+                for b0, b1 in banks_of(lo, hi):
+                    acc = psum.tile([P, b1 - b0], F32, name="acc%d_%d" % (m, b0))
+                    for c0, c1 in passes_of(b0, b1):
+                        nc.tensor.matmul_mx(
+                            out=acc[:, c0 - b0 : c1 - b0],
+                            lhsT=w8_code[:, rows].bitcast(FP8X4),
+                            lhsT_scale=w8_plane[:, rows],
+                            rhs=got0[:, c0:c1].bitcast(FP8X4),
+                            rhs_scale=planes[:, 0, c0:c1],
+                            start=True,
+                            stop=False,
+                        )
+                        nc.tensor.matmul_mx(
+                            out=acc[:, c0 - b0 : c1 - b0],
+                            lhsT=w4_code[:, 2 * m * P : 2 * (m + 1) * P].bitcast(FP4X4),
+                            lhsT_scale=w4_plane[:, rows],
+                            rhs=got1[h][:, c0 - lo : c1 - lo].bitcast(FP8X4),
+                            rhs_scale=planes[:, 1, c0:c1],
+                            start=False,
+                            stop=True,
+                        )
+                    nc.scalar.activation(
+                        y[:, b0 - lo : b1 - lo], acc[:], mybir.ActivationFunctionType.Identity, bias=bias[:, m : m + 1]
+                    )
                 nc.vector.tensor_tensor(
-                    pages[m][:].indirect(place[:, h * LCOL : (h + 1) * LCOL]),
+                    pages[m][:].indirect(place[:, lo // 16 : hi // 16]),
                     y[:],
-                    wgo_sb[:, cols],
+                    wgo_sb[:, lo:hi],
                     mybir.AluOpType.mult,
                 )
         for m in range(ROWT):

@@ -54,8 +54,7 @@ def tile_list_tabhs_o_bias_kernel(tc, tab, w8, w4_words, w4_scales, b, wgo, offs
         planes = keep.tile([P, 2, S], U8, name="planes", align_bytes=64)
         pages = [keep.tile([P, T], F32, name="page%d" % m, align_bytes=64) for m in range(ROWT)]
 
-        nc.vector.memset(tab_scale[32:64, :].bitcast(I32), 0)
-        nc.vector.memset(tab_scale[64:128, :].bitcast(I32), 0)
+        nc.vector.memset(tab_scale[0:96, :].bitcast(I32), 0)
         nc.gpsimd.memset(w4_plane[:].bitcast(I32), 0)
         nc.gpsimd.memset(planes[:].bitcast(I32), 0)
         nc.vector.memset(pages[0][:].bitcast(I32), 0)
@@ -69,7 +68,7 @@ def tile_list_tabhs_o_bias_kernel(tc, tab, w8, w4_words, w4_scales, b, wgo, offs
 
         nc.sync.dma_start(pick[:], offs)
         scale_rows = tab[:, WORD_BYTES:].bitcast(I32).rearrange("a (q c) -> q a c", q=QUADS * QROWS)
-        nc.sync.dma_start(tab_scale[0:32, :].bitcast(I32), scale_rows)
+        nc.sync.dma_start(tab_scale[96:128, :].bitcast(I32), scale_rows)
         nc.sync.dma_start(tab_words[0][:], words_of(0))
         nc.sync.dma_start(w8_raw[:], w8.rearrange("(p j) n -> p j n", j=PACK))
         nc.sync.dma_start(tab_words[1][:], words_of(1))
@@ -89,7 +88,7 @@ def tile_list_tabhs_o_bias_kernel(tc, tab, w8, w4_words, w4_scales, b, wgo, offs
         for q in range(QUADS):
             nc.sync.dma_start(
                 planes[32 * q : 32 * q + QROWS, :, :].bitcast(I32),
-                got_scale[2 * QROWS * q : 2 * QROWS * (q + 1), :].bitcast(I32),
+                got_scale[96 + 2 * QROWS * q : 96 + 2 * QROWS * (q + 1), :].bitcast(I32),
             )
 
         wgo_sb = keep.tile([P, S], F32, name="wgo_sb", tag="late", align_bytes=64)
@@ -116,16 +115,16 @@ def tile_list_tabhs_o_bias_kernel(tc, tab, w8, w4_words, w4_scales, b, wgo, offs
                 y = keep.tile([P, hi - lo], F32, name="y%d%d" % (h, m), align_bytes=64)
                 for b0, b1 in banks_of(lo, hi):
                     acc = psum.tile([P, b1 - b0], F32, name="acc%d_%d" % (m, b0))
+                    nc.tensor.matmul_mx(
+                        out=acc[:],
+                        lhsT=w8_code[:, rows].bitcast(FP8X4),
+                        lhsT_scale=w8_plane[:, rows],
+                        rhs=got0[:, b0:b1].bitcast(FP8X4),
+                        rhs_scale=planes[:, 0, b0:b1],
+                        start=True,
+                        stop=False,
+                    )
                     for c0, c1 in passes_of(b0, b1):
-                        nc.tensor.matmul_mx(
-                            out=acc[:, c0 - b0 : c1 - b0],
-                            lhsT=w8_code[:, rows].bitcast(FP8X4),
-                            lhsT_scale=w8_plane[:, rows],
-                            rhs=got0[:, c0:c1].bitcast(FP8X4),
-                            rhs_scale=planes[:, 0, c0:c1],
-                            start=True,
-                            stop=False,
-                        )
                         nc.tensor.matmul_mx(
                             out=acc[:, c0 - b0 : c1 - b0],
                             lhsT=w4_code[:, 2 * m * P : 2 * (m + 1) * P].bitcast(FP4X4),
@@ -133,7 +132,7 @@ def tile_list_tabhs_o_bias_kernel(tc, tab, w8, w4_words, w4_scales, b, wgo, offs
                             rhs=got1[h][:, c0 - lo : c1 - lo].bitcast(FP8X4),
                             rhs_scale=planes[:, 1, c0:c1],
                             start=False,
-                            stop=True,
+                            stop=(c1 == b1),
                         )
                     nc.scalar.activation(
                         y[:, b0 - lo : b1 - lo], acc[:], mybir.ActivationFunctionType.Identity, bias=bias[:, m : m + 1]

from contextlib import ExitStack

import concourse.mybir as mybir

K, M, T, S = 1024, 256, 2048, 1024
FLOPS = 2 * K * M * S

F32 = mybir.dt.float32
BF16 = mybir.dt.bfloat16
I32 = mybir.dt.int32
U32 = mybir.dt.uint32
U16 = mybir.dt.uint16
U8 = mybir.dt.uint8
FP8X4 = mybir.dt.float8_e4m3fn_x4
FP4X4 = mybir.dt.float4_e2m1fn_x4

P = 128
PACK = 4
QUADS = 4
QROWS = 4
N = 512
HALVES = S // N
ROWT = M // P
WORD_BYTES = P * PACK * T
SHORT = 128
CHUNKS = ((0, 256), (256, S))


def banks_of(lo, hi):
    return [(c, min(c + N, hi)) for c in range(lo, hi, N)]


def passes_of(lo, hi):
    step = N if hi - lo == N else SHORT
    return [(c, c + step) for c in range(lo, hi, step)]


def tile_list_tabhs_o_bias_kernel(tc, tab, w8, w4_words, w4_scales, b, wgo, offs, offs2, out):
    nc = tc.nc
    with ExitStack() as ctx:
        lists = ctx.enter_context(tc.tile_pool(name="lists", bufs=1))
        keep = ctx.enter_context(tc.tile_pool(name="keep", bufs=1))
        psum = ctx.enter_context(tc.psum_pool(name="psum", bufs=1))

        pick = lists.tile([P, S // 16], U16, name="pick")
        place = lists.tile([P, S // 16], U16, name="place")

        tab_scale = keep.tile([P, T], U8, name="tab_scale", tag="late", align_bytes=64)
        tab_words = [keep.tile([P, T], I32, name="tab_words%d" % a, align_bytes=64) for a in range(2)]
        w8_raw = keep.tile([P, PACK, M], F32, name="w8_raw", align_bytes=64)
        w4_code = keep.tile([P, 2 * M], U8, name="w4_code", align_bytes=64)
        w4_plane = keep.tile([P, M], U8, name="w4_plane", align_bytes=64)
        bias = keep.tile([P, ROWT], F32, name="bias", align_bytes=64)
        planes = keep.tile([P, 2, S], U8, name="planes", align_bytes=64)
        pages = [keep.tile([P, T], F32, name="page%d" % m, align_bytes=64) for m in range(ROWT)]

        nc.vector.memset(tab_scale[0:96, :].bitcast(I32), 0)
        nc.gpsimd.memset(w4_plane[:].bitcast(I32), 0)
        nc.gpsimd.memset(planes[:].bitcast(I32), 0)
        nc.vector.memset(pages[0][:].bitcast(I32), 0)

        warm = keep.tile([P, 2], F32, name="warm")
        nc.gpsimd.memset(warm[:, 0:1], 0.0)
        nc.scalar.activation(warm[:, 1:2], warm[:, 0:1], mybir.ActivationFunctionType.Identity, bias=warm[:, 0:1])

        def words_of(a):
            return tab[a, 0:WORD_BYTES].rearrange("(p t) -> p t", p=P).bitcast(I32)

        nc.sync.dma_start(pick[:], offs)
        scale_rows = tab[:, WORD_BYTES:].bitcast(I32).rearrange("a (q c) -> q a c", q=QUADS * QROWS)
        nc.sync.dma_start(tab_scale[96:128, :].bitcast(I32), scale_rows)
        nc.sync.dma_start(tab_words[0][:], words_of(0))
        nc.sync.dma_start(w8_raw[:], w8.rearrange("(p j) n -> p j n", j=PACK))
        nc.sync.dma_start(tab_words[1][:], words_of(1))
        nc.sync.dma_start(w4_code[:].bitcast(I32), w4_words[0].bitcast(I32))
        nc.sync.dma_start(place[:], offs2)
        for q in range(QUADS):
            nc.gpsimd.dma_start(
                w4_plane[32 * q : 32 * q + QROWS, :].bitcast(I32),
                w4_scales[0, QROWS * q : QROWS * (q + 1), :].bitcast(I32),
            )
        with nc.allow_non_contiguous_dma(reason="one bias value for each partition and row tile"):
            nc.gpsimd.dma_start(bias[:], b.rearrange("(m p) -> p m", p=P))
        nc.gpsimd.memset(pages[1][:].bitcast(I32), 0)

        got_scale = keep.tile([P, S], U8, name="got_scale", align_bytes=64)
        nc.vector.tensor_copy(got_scale[:], tab_scale[:].indirect(pick[:]))
        for q in range(QUADS):
            nc.sync.dma_start(
                planes[32 * q : 32 * q + QROWS, :, :].bitcast(I32),
                got_scale[96 + 2 * QROWS * q : 96 + 2 * QROWS * (q + 1), :].bitcast(I32),
            )

        wgo_sb = keep.tile([P, S], F32, name="wgo_sb", tag="late", align_bytes=64)
        nc.sync.dma_start(wgo_sb[:], wgo)

        got0 = keep.tile([P, S], U32, name="got0", align_bytes=64)
        nc.vector.tensor_copy(got0[:], tab_words[0][:].bitcast(U32).indirect(pick[:]))

        w8_bf = keep.tile([P, M, PACK], BF16, name="w8_bf", tag="shared", align_bytes=64)
        nc.scalar.copy(w8_bf[:], w8_raw[:].rearrange("p j n -> p n j"))
        w8_code = keep.tile([P, M], U32, name="w8_code", align_bytes=64)
        w8_plane = keep.tile([P, M], U8, name="w8_plane", align_bytes=64)
        nc.vector.quantize_mx(out=w8_code[:].bitcast(FP8X4), scales=w8_plane[:], in_=w8_bf[:].rearrange("p n j -> p (n j)"))

        got1 = []
        for h, (lo, hi) in enumerate(CHUNKS):
            g = keep.tile([P, hi - lo], U32, name="got1_%d" % h, tag="shared" if h == 0 else "got1_last", align_bytes=64)
            nc.vector.tensor_copy(g[:], tab_words[1][:].bitcast(U32).indirect(pick[:, lo // 16 : hi // 16]))
            got1.append(g)

        for h, (lo, hi) in enumerate(CHUNKS):
            for m in range(ROWT):
                rows = slice(m * P, (m + 1) * P)
                y = keep.tile([P, hi - lo], F32, name="y%d%d" % (h, m), align_bytes=64)
                for b0, b1 in banks_of(lo, hi):
                    acc = psum.tile([P, b1 - b0], F32, name="acc%d_%d" % (m, b0))
                    nc.tensor.matmul_mx(
                        out=acc[:],
                        lhsT=w8_code[:, rows].bitcast(FP8X4),
                        lhsT_scale=w8_plane[:, rows],
                        rhs=got0[:, b0:b1].bitcast(FP8X4),
                        rhs_scale=planes[:, 0, b0:b1],
                        start=True,
                        stop=False,
                    )
                    for c0, c1 in passes_of(b0, b1):
                        nc.tensor.matmul_mx(
                            out=acc[:, c0 - b0 : c1 - b0],
                            lhsT=w4_code[:, 2 * m * P : 2 * (m + 1) * P].bitcast(FP4X4),
                            lhsT_scale=w4_plane[:, rows],
                            rhs=got1[h][:, c0 - lo : c1 - lo].bitcast(FP8X4),
                            rhs_scale=planes[:, 1, c0:c1],
                            start=False,
                            stop=(c1 == b1),
                        )
                    nc.scalar.activation(
                        y[:, b0 - lo : b1 - lo], acc[:], mybir.ActivationFunctionType.Identity, bias=bias[:, m : m + 1]
                    )
                nc.vector.tensor_tensor(
                    pages[m][:].indirect(place[:, lo // 16 : hi // 16]),
                    y[:],
                    wgo_sb[:, lo:hi],
                    mybir.AluOpType.mult,
                )
        for m in range(ROWT):
            nc.sync.dma_start(out[m * P : (m + 1) * P, :], pages[m][:])
